import numpy as np
import ml_dtypes


def mxq(x, axis, fmt="e4m3"):
    dtype, down = {"e4m3": (ml_dtypes.float8_e4m3fn, 7), "e5m2": (ml_dtypes.float8_e5m2, 14)}[fmt]
    v = np.moveaxis(np.asarray(x, np.float32).astype(ml_dtypes.bfloat16).astype(np.float64), axis, -1)
    blocks = v.reshape(v.shape[:-1] + (-1, 32))
    amax = np.abs(blocks).max(-1, keepdims=True)
    byte = np.maximum(np.where(amax > 0, np.frexp(amax)[1] - 1 + 127, 0) - down, 1)
    scale = np.exp2(byte - 127.0)
    codes = (blocks / scale).astype(np.float32).astype(dtype).astype(np.float64)
    return np.moveaxis((codes * scale).reshape(v.shape), -1, axis)


WIDE = False


def mx_kscale(k):
    if not WIDE:
        return np.ones(k)
    levels = np.array([10, -10, 5, -5, 0])
    if k % 512:
        return np.exp2(np.random.permutation(np.resize(levels, k // 32))).repeat(32)
    a = np.empty((k // 512, 16))
    for p in range(k // 512):
        a[p, :8] = np.random.permutation(np.resize(levels, 8))
        for g in range(8):
            far = levels[np.abs(levels - a[p, g]) >= 10]
            a[p, g + 8] = far[np.random.randint(len(far))]
    return np.exp2(a.ravel()).repeat(32)


BF16 = ml_dtypes.bfloat16


def bf(x):
    return np.asarray(x, np.float32).astype(BF16)


def f64(x):
    return np.asarray(x).astype(np.float64)


E2M1 = np.array([0.0, 0.5, 1.0, 1.5, 2.0, 3.0, 4.0, 6.0, -0.0, -0.5, -1.0, -1.5, -2.0, -3.0, -4.0, -6.0])


def pack_weight(w, fmt):
    k, n = w.shape
    w = f64(bf(w)).reshape(k // 32, 32, n)
    amax = np.abs(w).max(1)
    if fmt == "e4m3":
        byte = np.frexp(amax)[1] - 1 + 127 - 7
    else:
        mant, ex = np.frexp(amax / 6.0)
        byte = np.where(mant > 0.5, ex, ex - 1) + 127
    byte = np.clip(np.where(amax > 0, byte, 1), 1, 254)
    scaled = (w * np.exp2(127.0 - byte)[:, None, :]).reshape(k, n).astype(np.float32)
    by_word = np.ascontiguousarray(scaled.reshape(k // 512, 128, 4, n).transpose(0, 1, 3, 2))
    if fmt == "e4m3":
        words = by_word.astype(ml_dtypes.float8_e4m3fn).view(np.uint8)
    else:
        c = by_word.astype(ml_dtypes.float4_e2m1fn).view(np.uint8) & 0xF
        words = c[..., 0::2] | (c[..., 1::2] << 4)
    return np.ascontiguousarray(words), np.ascontiguousarray(byte.astype(np.uint8).reshape(k // 512, 16, n))


def unpack_weight(words, scales, fmt):
    g, p, n, _ = words.shape
    if fmt == "e4m3":
        vals = np.ascontiguousarray(words).view(ml_dtypes.float8_e4m3fn).astype(np.float64)
    else:
        nib = np.empty((g, p, n, 4), np.uint8)
        nib[..., 0::2] = words & 0xF
        nib[..., 1::2] = words >> 4
        vals = E2M1[nib]
    vals = vals * np.repeat(np.exp2(scales.astype(np.float64) - 127.0), 8, axis=1)[..., None]
    return vals.transpose(0, 1, 3, 2).reshape(g * 512, n)
def pack4(w):
    words, scales = pack_weight(w, "e2m1")
    return words.reshape(words.shape[0], 128, -1), scales


def unpack4(words, scales):
    return unpack_weight(words.reshape(words.shape[0], 128, -1, 2), scales, "e2m1")


def planes(Y):
    n, m = Y.shape
    b = f64(bf(Y)).reshape(n // 32, 32, m)
    amax = np.abs(b).max(1)
    byte = np.clip(np.where(amax > 0, np.frexp(amax)[1] - 1 + 127 - 7, 1), 1, 254)
    codes = (b * np.exp2(127.0 - byte)[:, None, :]).reshape(n, m).astype(np.float32).astype(ml_dtypes.float8_e4m3fn).view(np.uint8)
    words = codes.reshape(n // 512, 128, 4, m).transpose(0, 1, 3, 2)
    return np.ascontiguousarray(words), np.ascontiguousarray(byte.astype(np.uint8).reshape(n // 512, 16, m))


G, R, S, Z, D = 4, 512, 1024, 1024, 512
LIMIT, SOFT = 10.0, 1.5


def setup_inputs():
    n = np.random.randn
    s = mx_kscale(G * S).reshape(G, S)
    t = mx_kscale(G * Z).reshape(G, Z)
    moves = n(G, R, S) * 2.5 / np.sqrt(S) * s[:, None, :]
    travel = 12.0 * np.exp(0.5 * n(G, S, Z))
    kern = 1.0 / (1.0 + np.exp((travel - LIMIT) / SOFT)) / s[:, :, None]
    weight = n(G, Z, D) * np.exp(0.8 * n(G, 1, D)) / np.sqrt(Z) / t[:, :, None]
    kern_words, kern_scales = pack4(kern.reshape(G * S, Z))
    weight_words, weight_scales = pack4(weight.reshape(G * Z, D))
    return {"moves": bf(moves), "kern_words": kern_words, "kern_scales": kern_scales,
            "demand": bf(np.exp(0.4 * n(G, Z)) * t),
            "weight_words": weight_words, "weight_scales": weight_scales,
            "staffing": bf(np.random.uniform(0.5, 1.0, (G, R))),
            "offset": bf(0.4 * n(G, D))}


def reference(moves, kern_words, kern_scales, demand, weight_words, weight_scales, staffing, offset):
    W = unpack4(kern_words, kern_scales).reshape(G, S, Z)
    V = unpack4(weight_words, weight_scales).reshape(G, Z, D)
    a = mxq(f64(moves), 2) @ W
    h = f64(demand)[:, None, :] * (1.0 / (1.0 + np.exp(-a)))
    c = mxq(h, 2) @ V
    y = f64(staffing)[:, :, None] * c + f64(offset)[:, None, :]
    Y = y.transpose(2, 0, 1).reshape(D, G * R)
    words, scales = planes(Y)
    return y, words, scales

@@ -1,0 +1,274 @@
+from contextlib import ExitStack
+
+import concourse.mybir as mybir
+from concourse.masks import make_identity
+
+G, R, S, Z, D = 4, 512, 1024, 1024, 512
+FLOPS = 2 * G * R * (S * Z + Z * D)
+
+F32 = mybir.dt.float32
+BF16 = mybir.dt.bfloat16
+I32 = mybir.dt.int32
+U32 = mybir.dt.uint32
+U8 = mybir.dt.uint8
+FP8X4 = mybir.dt.float8_e4m3fn_x4
+FP4X4 = mybir.dt.float4_e2m1fn_x4
+ACT = mybir.ActivationFunctionType
+ALU = mybir.AluOpType
+
+P = 128
+BANK = 512
+TILES = R // P
+UNITS = G * TILES
+PASSES = 2
+
+
+def tile_ambulance_expected_coverage_k7_kernel(
+    tc, moves, kern_words, kern_scales, demand, weight_words, weight_scales, staffing, offset, out_0, out_1, out_2
+):
+    nc = tc.nc
+    with ExitStack() as ctx:
+        keep = ctx.enter_context(tc.tile_pool(name="keep", bufs=1))
+        work = ctx.enter_context(tc.tile_pool(name="work", bufs=3))
+        psum = ctx.enter_context(tc.psum_pool(name="psum", bufs=1))
+        ctx.enter_context(tc.manual_schedule())
+
+        ident = keep.tile([P, P], F32)
+        mv = keep.tile([P, UNITS, S], BF16, align_bytes=64)
+        w_words = keep.tile([P, G * PASSES, 2 * Z], U8, align_bytes=64)
+        w_scales = keep.tile([P, G * PASSES, Z], U8, align_bytes=64)
+        v_words = keep.tile([P, G * PASSES, 2 * D], U8, align_bytes=64)
+        v_scales = keep.tile([P, G * PASSES, D], U8, align_bytes=64)
+        demand_all = keep.tile([P, G, Z], BF16, align_bytes=64)
+        offset_all = keep.tile([P, G, D], BF16, align_bytes=64)
+        staff_rows = keep.tile([UNITS, P], BF16)
+        staff_wide = keep.tile([P, P], F32)
+        staff_cols = keep.tile([P, UNITS], F32)
+        y = keep.tile([P, UNITS, D], F32, align_bytes=64)
+        y_codes = keep.tile([P, G * R], U32, align_bytes=64)
+        y_scales = keep.tile([P, G * R], U8, align_bytes=64)
+
+        def clear(plane, passes):
+            nc.vector.memset(plane[:, passes, :].rearrange("p g n -> p (g n)").bitcast(I32), 0)
+
+        def load_scales(plane, rows, passes):
+            for q in range(4):
+                nc.sync.dma_start(
+                    out=plane[32 * q : 32 * q + 4, passes, :].bitcast(I32),
+                    in_=rows[passes, 4 * q : 4 * q + 4, :].rearrange("g r n -> r g n").bitcast(I32),
+                )
+
+        def load_words(words, rows, passes):
+            nc.sync.dma_start(
+                out=words[:, passes, :].bitcast(I32), in_=rows[passes].rearrange("g p n -> p g n").bitcast(I32)
+            )
+
+        def load_moves(first, count):
+            rows = moves.rearrange("i (j p) s -> p (i j) s", p=P)
+            nc.sync.dma_start(out=mv[:, first : first + count, :], in_=rows[:, first : first + count, :])
+
+        def spread(dst, src, shifts):
+            nc.sync.dma_start(
+                out=dst[:, shifts, :].rearrange("p i n -> p (i n)"),
+                in_=src[shifts, :].rearrange("i n -> (i n)").partition_broadcast(P),
+            )
+
+        first, rest, every = slice(0, PASSES), slice(PASSES, G * PASSES), slice(0, G * PASSES)
+        make_identity(nc, ident[:])
+        clear(w_scales, first)
+        clear(v_scales, every)
+        nc.vector.memset(staff_wide[:], 0.0)
+        clear(w_scales, rest)
+
+        load_moves(0, 1)
+        load_scales(w_scales, kern_scales, first)
+        load_words(w_words, kern_words, slice(0, 1))
+        load_words(w_words, kern_words, slice(1, 2))
+        load_moves(1, 1)
+        nc.sync.dma_start(out=staff_rows[:], in_=staffing.rearrange("i (j p) -> (i j) p", p=P))
+        spread(demand_all, demand, slice(0, 1))
+        load_moves(2, 1)
+        load_scales(v_scales, weight_scales, every)
+        load_words(v_words, weight_words, first)
+        load_moves(3, 1)
+        spread(offset_all, offset, slice(0, G))
+        load_scales(w_scales, kern_scales, rest)
+        for i in range(1, G):
+            load_moves(TILES * i, TILES)
+            load_words(w_words, kern_words, slice(PASSES * i, PASSES * i + PASSES))
+            if i == 1:
+                spread(demand_all, demand, slice(1, G))
+            load_words(v_words, weight_words, slice(PASSES * i, PASSES * i + PASSES))
+
+        t = {}
+
+        def T1(u):
+            bank = psum.tile([P, PASSES, 2, P], F32, name="x_bank")
+            words = mv[:, u, :].bitcast(F32)
+            for g in range(PASSES):
+                for h in range(2):
+                    nc.tensor.transpose(bank[:, g, h, :], words[:, 256 * g + h : 256 * (g + 1) : 2], ident[:])
+            t["x_bank", u] = bank
+
+        def evac(engine, dst, bank):
+            src = bank[:].rearrange("p g h r -> p g r h")
+            dst = dst[:].bitcast(F32).rearrange("p (g r h) -> p g r h", g=2, h=2)
+            if engine == "vector":
+                nc.vector.tensor_copy(out=dst, in_=src)
+            else:
+                nc.scalar.copy(out=dst, in_=src)
+
+        def e1(u):
+            xt = work.tile([P, S], BF16, name="xt", align_bytes=64)
+            evac("vector" if u < 2 else "scalar", xt, t["x_bank", u])
+            t["xt", u] = xt
+
+        def quant(name, src):
+            codes = work.tile([P, PASSES * P], U32, name=name + "_codes", align_bytes=64)
+            scales = work.tile([P, PASSES * P], U8, name=name + "_scales", align_bytes=64)
+            nc.vector.quantize_mx(out=codes[:].bitcast(FP8X4), scales=scales[:], in_=src[:])
+            return codes, scales
+
+        def q1(u):
+            t["xq", u] = quant("x", t["xt", u])
+
+        def product(bank, quantised, words, scales, shift, cols):
+            codes, code_scales = quantised
+            for g in range(PASSES):
+                k = PASSES * shift + g
+                nc.tensor.matmul_mx(
+                    out=bank[:],
+                    lhsT=codes[:, P * g : P * (g + 1)].bitcast(FP8X4),
+                    lhsT_scale=code_scales[:, P * g : P * (g + 1)],
+                    rhs=words[:, k, 2 * cols.start : 2 * cols.stop].bitcast(FP4X4),
+                    rhs_scale=scales[:, k, cols],
+                    start=(g == 0),
+                    stop=(g == PASSES - 1),
+                )
+
+        def M1(u, half):
+            bank = psum.tile([P, BANK], F32, name="a_bank", bufs=4)
+            product(bank, t["xq", u], w_words, w_scales, u // TILES, slice(BANK * half, BANK * (half + 1)))
+            t["a_bank", u, half] = bank
+
+        def sig(u, half):
+            if half == 0:
+                t["sig", u] = work.tile([P, 2, PASSES, P, 2], F32, name="sig", align_bytes=64)
+            nc.scalar.activation(
+                out=t["sig", u][:, :, half, :, :],
+                in_=t["a_bank", u, half][:].rearrange("r (p h e) -> r h p e", h=2, e=2),
+                func=ACT.Sigmoid,
+            )
+
+        def mult(u):
+            hb = work.tile([P, Z], BF16, name="hb", align_bytes=64)
+            nc.vector.tensor_tensor(
+                out=hb[:].rearrange("r (h q e) -> r h q e", h=2, e=2),
+                in0=t["sig", u][:].rearrange("r h g p e -> r h (g p) e"),
+                in1=demand_all[:, u // TILES, :].rearrange("r (q h e) -> r h q e", h=2, e=2),
+                op=ALU.mult,
+            )
+            t["hb", u] = hb
+
+        def T2(u):
+            bank = psum.tile([P, PASSES, 2, P], F32, name="h_bank")
+            words = t["hb", u][:].bitcast(F32)
+            for g in range(PASSES):
+                for h in range(2):
+                    c = 256 * h + P * g
+                    nc.tensor.transpose(bank[:, g, h, :], words[:, c : c + P], ident[:])
+            t["h_bank", u] = bank
+
+        def e2(u):
+            ht = work.tile([P, Z], BF16, name="ht", align_bytes=64)
+            evac("scalar", ht, t["h_bank", u])
+            t["ht", u] = ht
+
+        def q2(u):
+            t["hq", u] = quant("h", t["ht", u])
+
+        def M2(u):
+            bank = psum.tile([P, BANK], F32, name="c_bank")
+            product(bank, t["hq", u], v_words, v_scales, u // TILES, slice(0, D))
+            t["c_bank", u] = bank
+
+        def staff():
+            nc.vector.tensor_copy(out=staff_wide[0:UNITS, :], in_=staff_rows[:])
+            bank = psum.tile([P, 2, 2, P], F32, name="y_bank")
+            nc.tensor.transpose(bank[:, 0, 0, :], staff_wide[:], ident[:])
+            nc.vector.tensor_copy(out=staff_cols[:], in_=bank[:, 0, 0, 0:UNITS])
+
+        def yy(u):
+            nc.vector.scalar_tensor_tensor(
+                out=y[:, u, :],
+                in0=t["c_bank", u][:],
+                scalar=staff_cols[:, u : u + 1],
+                in1=offset_all[:, u // TILES, :],
+                op0=ALU.mult,
+                op1=ALU.add,
+            )
+            rows = out_0.rearrange("i (j p) d -> p (i j) d", p=P)
+            nc.sync.dma_start(out=rows[:, u, :], in_=y[:, u, :])
+
+        def cast(u):
+            yb = work.tile([P, D], BF16, name="yb", align_bytes=64)
+            dst = yb[:].rearrange("r (h p e) -> r h p e", h=2, e=2)
+            src = y[:, u, :].rearrange("r (p h e) -> r h p e", h=2, e=2)
+            if True:
+                nc.vector.tensor_copy(out=dst, in_=src)
+            else:
+                nc.scalar.copy(out=dst, in_=src)
+            t["yb", u] = yb
+
+        def T3(u):
+            if u % 2 == 0:
+                t["y_bank"] = psum.tile([P, 2, 2, P], F32, name="y_bank")
+            words = t["yb", u][:].bitcast(F32)
+            for h in range(2):
+                nc.tensor.transpose(t["y_bank"][:, u % 2, h, :], words[:, P * h : P * (h + 1)], ident[:])
+
+        def e3(u):
+            if u % 2 == 1:
+                yt = work.tile([P, 2 * D], BF16, name="yt", align_bytes=64)
+                evac("scalar", yt, t["y_bank"])
+                t["yt", u] = yt
+
+        def q3(u):
+            if u % 2 == 1:
+                cols = slice(P * (u - 1), P * (u + 1))
+                nc.vector.quantize_mx(out=y_codes[:, cols].bitcast(FP8X4), scales=y_scales[:, cols], in_=t["yt", u][:])
+                words = out_1[0].rearrange("p m t -> p (m t)").bitcast(I32)
+                nc.sync.dma_start(out=words[:, cols], in_=y_codes[:, cols].bitcast(I32))
+            if u % TILES == TILES - 1:
+                cols = slice(R * (u // TILES), R * (u // TILES + 1))
+                for q in range(4):
+                    nc.sync.dma_start(
+                        out=out_2[0, 4 * q : 4 * q + 4, cols].bitcast(I32),
+                        in_=y_scales[32 * q : 32 * q + 4, cols].bitcast(I32),
+                    )
+
+        order = [
+            (T1, 0),
+            (T2, 3),
+            (T3, 6),
+            (mult, 2),
+            (e1, 0),
+            (q1, 0),
+            (e2, 3),
+            (e3, 6),
+            (q2, 3),
+            (lambda u: M1(u, 0), 1),
+            (lambda u: sig(u, 0), 1),
+            (lambda u: M1(u, 1), 1),
+            (lambda u: sig(u, 1), 1),
+            (cast, 5),
+            (M2, 4),
+            (yy, 4),
+            (q3, 6),
+        ]
+        for step in range(UNITS + max(lag for stage, lag in order)):
+            if step == 2:
+                staff()
+            for stage, lag in order:
+                if 0 <= step - lag < UNITS:
+                    stage(step - lag)

@@ -41,9 +41,9 @@ def tile_ambulance_expected_coverage_k7_kernel(
         v_scales = keep.tile([P, G * PASSES, D], U8, align_bytes=64)
         demand_all = keep.tile([P, G, Z], BF16, align_bytes=64)
         offset_all = keep.tile([P, G, D], BF16, align_bytes=64)
-        staff_rows = keep.tile([UNITS, P], BF16)
-        staff_wide = keep.tile([P, P], F32)
-        staff_cols = keep.tile([P, UNITS], F32)
+        demand_cols = keep.tile([P, G, 8], BF16)
+        offset_cols = keep.tile([P, G, 4], BF16)
+        staff_cols = keep.tile([P, UNITS // 2, 2], BF16)
         y = keep.tile([P, UNITS, D], F32, align_bytes=64)
         y_codes = keep.tile([P, G * R], U32, align_bytes=64)
         y_scales = keep.tile([P, G * R], U8, align_bytes=64)
@@ -64,40 +64,37 @@ def tile_ambulance_expected_coverage_k7_kernel(
             )
 
         def load_moves(first, count):
-            rows = moves.rearrange("i (j p) s -> p (i j) s", p=P)
-            nc.sync.dma_start(out=mv[:, first : first + count, :], in_=rows[:, first : first + count, :])
-
-        def spread(dst, src, shifts):
-            nc.sync.dma_start(
-                out=dst[:, shifts, :].rearrange("p i n -> p (i n)"),
-                in_=src[shifts, :].rearrange("i n -> (i n)").partition_broadcast(P),
-            )
+            rows = moves.rearrange("i (a p j) s -> p (i a) j s", p=P, j=2)
+            if count == 1:
+                nc.sync.dma_start(out=mv[:, first, :], in_=rows[:, first // 2, first % 2, :])
+            else:
+                nc.sync.dma_start(
+                    out=mv[:, first : first + count, :].rearrange("p (a j) s -> p a (j s)", j=2),
+                    in_=rows[:, first // 2 : (first + count) // 2].rearrange("p a j s -> p a (j s)"),
+                )
 
         first, rest, every = slice(0, PASSES), slice(PASSES, G * PASSES), slice(0, G * PASSES)
         make_identity(nc, ident[:])
         clear(w_scales, first)
         clear(v_scales, every)
-        nc.vector.memset(staff_wide[:], 0.0)
         clear(w_scales, rest)
 
         load_moves(0, 1)
+        nc.scalar.dma_start(out=demand_cols[:], in_=demand.rearrange("i (k a) -> k i a", k=P))
+        nc.scalar.dma_start(out=offset_cols[:], in_=offset.rearrange("i (k a) -> k i a", k=P))
+        nc.scalar.dma_start(out=staff_cols[:], in_=staffing.rearrange("i (a p j) -> p (i a) j", p=P, j=2))
         load_scales(w_scales, kern_scales, first)
         load_words(w_words, kern_words, slice(0, 1))
         load_words(w_words, kern_words, slice(1, 2))
         load_moves(1, 1)
-        nc.sync.dma_start(out=staff_rows[:], in_=staffing.rearrange("i (j p) -> (i j) p", p=P))
-        spread(demand_all, demand, slice(0, 1))
         load_moves(2, 1)
         load_scales(v_scales, weight_scales, every)
         load_words(v_words, weight_words, first)
         load_moves(3, 1)
-        spread(offset_all, offset, slice(0, G))
         load_scales(w_scales, kern_scales, rest)
         for i in range(1, G):
             load_moves(TILES * i, TILES)
             load_words(w_words, kern_words, slice(PASSES * i, PASSES * i + PASSES))
-            if i == 1:
-                spread(demand_all, demand, slice(1, G))
             load_words(v_words, weight_words, slice(PASSES * i, PASSES * i + PASSES))
 
         t = {}
@@ -111,8 +108,13 @@ def tile_ambulance_expected_coverage_k7_kernel(
             t["x_bank", u] = bank
 
         def evac(engine, dst, bank):
-            src = bank[:].rearrange("p g h r -> p g r h")
-            dst = dst[:].bitcast(F32).rearrange("p (g r h) -> p g r h", g=2, h=2)
+            copy_words(
+                engine,
+                dst.bitcast(F32).rearrange("p (g r h) -> p g r h", g=2, h=2),
+                bank[:].rearrange("p g h r -> p g r h"),
+            )
+
+        def copy_words(engine, dst, src):
             if engine == "vector":
                 nc.vector.tensor_copy(out=dst, in_=src)
             else:
@@ -120,7 +122,7 @@ def tile_ambulance_expected_coverage_k7_kernel(
 
         def e1(u):
             xt = work.tile([P, S], BF16, name="xt", align_bytes=64)
-            evac("vector" if u < 2 else "scalar", xt, t["x_bank", u])
+            evac("vector" if u < 2 else "scalar", xt[:], t["x_bank", u])
             t["xt", u] = xt
 
         def quant(name, src):
@@ -163,9 +165,9 @@ def tile_ambulance_expected_coverage_k7_kernel(
         def mult(u):
             hb = work.tile([P, Z], BF16, name="hb", align_bytes=64)
             nc.vector.tensor_tensor(
-                out=hb[:].rearrange("r (h q e) -> r h q e", h=2, e=2),
-                in0=t["sig", u][:].rearrange("r h g p e -> r h (g p) e"),
-                in1=demand_all[:, u // TILES, :].rearrange("r (q h e) -> r h q e", h=2, e=2),
+                out=hb[:],
+                in0=t["sig", u][:].rearrange("r h g p e -> r (h g p e)"),
+                in1=demand_all[:, u // TILES, :],
                 op=ALU.mult,
             )
             t["hb", u] = hb
@@ -181,7 +183,7 @@ def tile_ambulance_expected_coverage_k7_kernel(
 
         def e2(u):
             ht = work.tile([P, Z], BF16, name="ht", align_bytes=64)
-            evac("scalar", ht, t["h_bank", u])
+            evac("scalar", ht[:], t["h_bank", u])
             t["ht", u] = ht
 
         def q2(u):
@@ -192,23 +194,35 @@ def tile_ambulance_expected_coverage_k7_kernel(
             product(bank, t["hq", u], v_words, v_scales, u // TILES, slice(0, D))
             t["c_bank", u] = bank
 
-        def staff():
-            nc.vector.tensor_copy(out=staff_wide[0:UNITS, :], in_=staff_rows[:])
-            bank = psum.tile([P, 2, 2, P], F32, name="y_bank")
-            nc.tensor.transpose(bank[:, 0, 0, :], staff_wide[:], ident[:])
-            nc.vector.tensor_copy(out=staff_cols[:], in_=bank[:, 0, 0, 0:UNITS])
+        def spread(cols, tag):
+            bank = psum.tile([P, 2, 2, P], F32, name=tag)
+            for c in range(4):
+                nc.tensor.transpose(bank[:, c // 2, c % 2, :], cols[:, c : c + 1].to_broadcast([P, P]), ident[:])
+            return bank
+
+        def spread_demand(i, tag, engine):
+            bank = spread(demand_cols[:, i, :].bitcast(F32), tag)
+            return lambda: copy_words(
+                engine,
+                demand_all[:, i, :].bitcast(F32).rearrange("p (h k a) -> p h k a", h=2, a=2),
+                bank[:].rearrange("p a h k -> p h k a"),
+            )
+
+        def spread_offset(i, tag, engine):
+            bank = spread(offset_cols[:, i : i + 2, :].rearrange("p i a -> p (i a)").bitcast(F32), tag)
+            return lambda: evac(engine, offset_all[:, i : i + 2, :].rearrange("p i d -> p (i d)"), bank)
 
         def yy(u):
             nc.vector.scalar_tensor_tensor(
                 out=y[:, u, :],
                 in0=t["c_bank", u][:],
-                scalar=staff_cols[:, u : u + 1],
+                scalar=staff_cols[:, u // 2, u % 2 : u % 2 + 1],
                 in1=offset_all[:, u // TILES, :],
                 op0=ALU.mult,
                 op1=ALU.add,
             )
-            rows = out_0.rearrange("i (j p) d -> p (i j) d", p=P)
-            nc.sync.dma_start(out=rows[:, u, :], in_=y[:, u, :])
+            rows = out_0.rearrange("i (a p j) d -> p (i a) j d", p=P, j=2)
+            nc.sync.dma_start(out=rows[:, u // 2, u % 2, :], in_=y[:, u, :])
 
         def cast(u):
             yb = work.tile([P, D], BF16, name="yb", align_bytes=64)
@@ -230,7 +244,11 @@ def tile_ambulance_expected_coverage_k7_kernel(
         def e3(u):
             if u % 2 == 1:
                 yt = work.tile([P, 2 * D], BF16, name="yt", align_bytes=64)
-                evac("scalar", yt, t["y_bank"])
+                copy_words(
+                    "scalar",
+                    yt[:].bitcast(F32).rearrange("p (r j h) -> p r j h", j=2, h=2),
+                    t["y_bank"][:].rearrange("p j h r -> p r j h"),
+                )
                 t["yt", u] = yt
 
         def q3(u):
@@ -267,8 +285,21 @@ def tile_ambulance_expected_coverage_k7_kernel(
             (q3, 6),
         ]
         for step in range(UNITS + max(lag for stage, lag in order)):
-            if step == 2:
-                staff()
+            late = []
             for stage, lag in order:
                 if 0 <= step - lag < UNITS:
                     stage(step - lag)
+                if stage is T1 and step in (0, 1, 2):
+                    engine = "vector" if step < 2 else "scalar"
+                    if step == 0:
+                        late = [spread_demand(0, "h_bank", engine)]
+                    elif step == 1:
+                        late = [spread_offset(0, "c_bank", engine), spread_demand(1, "y_bank", engine)]
+                    else:
+                        late = [
+                            spread_demand(2, "h_bank", engine),
+                            spread_offset(2, "c_bank", engine),
+                            spread_demand(3, "y_bank", engine),
+                        ]
+            for copy in late:
+                copy()

@@ -29,7 +29,7 @@ def tile_ambulance_expected_coverage_k7_kernel(
     nc = tc.nc
     with ExitStack() as ctx:
         keep = ctx.enter_context(tc.tile_pool(name="keep", bufs=1))
-        work = ctx.enter_context(tc.tile_pool(name="work", bufs=3))
+        work = ctx.enter_context(tc.tile_pool(name="work", bufs=6))
         psum = ctx.enter_context(tc.psum_pool(name="psum", bufs=1))
         ctx.enter_context(tc.manual_schedule())
 
@@ -58,9 +58,10 @@ def tile_ambulance_expected_coverage_k7_kernel(
                     in_=rows[passes, 4 * q : 4 * q + 4, :].rearrange("g r n -> r g n").bitcast(I32),
                 )
 
-        def load_words(words, rows, passes):
+        def load_words(words, rows, passes, cols=slice(None)):
             nc.sync.dma_start(
-                out=words[:, passes, :].bitcast(I32), in_=rows[passes].rearrange("g p n -> p g n").bitcast(I32)
+                out=words[:, passes, cols].bitcast(I32),
+                in_=rows[passes].rearrange("g p n -> p g n")[:, :, cols].bitcast(I32),
             )
 
         def load_moves(first, count):
@@ -73,34 +74,55 @@ def tile_ambulance_expected_coverage_k7_kernel(
                     in_=rows[:, first // 2 : (first + count) // 2].rearrange("p a j s -> p a (j s)"),
                 )
 
-        first, rest, every = slice(0, PASSES), slice(PASSES, G * PASSES), slice(0, G * PASSES)
+        def shifts(first, last):
+            return slice(PASSES * first, PASSES * (last + 1))
+
         make_identity(nc, ident[:])
-        clear(w_scales, first)
-        clear(v_scales, every)
-        clear(w_scales, rest)
+        clear(w_scales, shifts(0, 0))
+        clear(v_scales, shifts(0, 3))
+        clear(w_scales, shifts(1, 3))
 
         load_moves(0, 1)
-        nc.scalar.dma_start(out=demand_cols[:], in_=demand.rearrange("i (k a) -> k i a", k=P))
-        nc.scalar.dma_start(out=offset_cols[:], in_=offset.rearrange("i (k a) -> k i a", k=P))
-        nc.scalar.dma_start(out=staff_cols[:], in_=staffing.rearrange("i (a p j) -> p (i a) j", p=P, j=2))
-        load_scales(w_scales, kern_scales, first)
-        load_words(w_words, kern_words, slice(0, 1))
-        load_words(w_words, kern_words, slice(1, 2))
         load_moves(1, 1)
+        nc.sync.dma_start(out=demand_cols[:], in_=demand.rearrange("i (k a) -> k i a", k=P))
+        load_scales(w_scales, kern_scales, shifts(0, 0))
+        load_words(w_words, kern_words, shifts(0, 0), slice(0, Z))
+        load_words(w_words, kern_words, shifts(0, 0), slice(Z, 2 * Z))
         load_moves(2, 1)
-        load_scales(v_scales, weight_scales, every)
-        load_words(v_words, weight_words, first)
         load_moves(3, 1)
-        load_scales(w_scales, kern_scales, rest)
-        for i in range(1, G):
-            load_moves(TILES * i, TILES)
-            load_words(w_words, kern_words, slice(PASSES * i, PASSES * i + PASSES))
-            load_words(v_words, weight_words, slice(PASSES * i, PASSES * i + PASSES))
+        nc.sync.dma_start(out=offset_cols[:], in_=offset.rearrange("i (k a) -> k i a", k=P))
+        load_moves(4, 2)
+        load_scales(w_scales, kern_scales, shifts(1, 1))
+        load_words(w_words, kern_words, shifts(1, 1))
+        nc.sync.dma_start(out=staff_cols[:], in_=staffing.rearrange("i (a p j) -> p (i a) j", p=P, j=2))
+        load_scales(v_scales, weight_scales, shifts(0, 1))
+        load_words(v_words, weight_words, shifts(0, 0))
+        load_moves(6, 2)
+        load_moves(8, 4)
+        load_scales(w_scales, kern_scales, shifts(2, 3))
+        load_words(w_words, kern_words, shifts(2, 2))
+        load_words(v_words, weight_words, shifts(1, 1))
+        load_moves(12, 4)
+        load_words(w_words, kern_words, shifts(3, 3))
+        load_scales(v_scales, weight_scales, shifts(2, 3))
+        load_words(v_words, weight_words, shifts(2, 3))
+
+        taken = []
+
+        def next_bank(shape):
+            bank = psum.tile(shape, F32, name="bank%d" % (len(taken) % 8))
+            taken.append(bank)
+            return bank
+
+        on_vector = {"e1": [0,3],"e2": [],"e3": [],"c": [1,3,5,7,9,11,13,15],"eb": [0,1,2,4,5]}
+
+        def engine_of(stage, u):
+            return "vector" if u in on_vector[stage] else "scalar"
 
         t = {}
 
         def T1(u):
-            bank = psum.tile([P, PASSES, 2, P], F32, name="x_bank")
+            bank = next_bank([P, PASSES, 2, P])
             words = mv[:, u, :].bitcast(F32)
             for g in range(PASSES):
                 for h in range(2):
@@ -122,7 +144,7 @@ def tile_ambulance_expected_coverage_k7_kernel(
 
         def e1(u):
             xt = work.tile([P, S], BF16, name="xt", align_bytes=64)
-            evac("vector" if u < 2 else "scalar", xt[:], t["x_bank", u])
+            evac(engine_of("e1", u), xt[:], t["x_bank", u])
             t["xt", u] = xt
 
         def quant(name, src):
@@ -149,7 +171,7 @@ def tile_ambulance_expected_coverage_k7_kernel(
                 )
 
         def M1(u, half):
-            bank = psum.tile([P, BANK], F32, name="a_bank", bufs=4)
+            bank = next_bank([P, BANK])
             product(bank, t["xq", u], w_words, w_scales, u // TILES, slice(BANK * half, BANK * (half + 1)))
             t["a_bank", u, half] = bank
 
@@ -163,7 +185,7 @@ def tile_ambulance_expected_coverage_k7_kernel(
             )
 
         def mult(u):
-            hb = work.tile([P, Z], BF16, name="hb", align_bytes=64)
+            hb = work.tile([P, Z], BF16, name="hb", bufs=7, align_bytes=64)
             nc.vector.tensor_tensor(
                 out=hb[:],
                 in0=t["sig", u][:].rearrange("r h g p e -> r (h g p e)"),
@@ -173,7 +195,7 @@ def tile_ambulance_expected_coverage_k7_kernel(
             t["hb", u] = hb
 
         def T2(u):
-            bank = psum.tile([P, PASSES, 2, P], F32, name="h_bank")
+            bank = next_bank([P, PASSES, 2, P])
             words = t["hb", u][:].bitcast(F32)
             for g in range(PASSES):
                 for h in range(2):
@@ -183,34 +205,40 @@ def tile_ambulance_expected_coverage_k7_kernel(
 
         def e2(u):
             ht = work.tile([P, Z], BF16, name="ht", align_bytes=64)
-            evac("scalar", ht[:], t["h_bank", u])
+            evac(engine_of("e2", u), ht[:], t["h_bank", u])
             t["ht", u] = ht
 
         def q2(u):
             t["hq", u] = quant("h", t["ht", u])
 
         def M2(u):
-            bank = psum.tile([P, BANK], F32, name="c_bank")
+            bank = next_bank([P, BANK])
             product(bank, t["hq", u], v_words, v_scales, u // TILES, slice(0, D))
             t["c_bank", u] = bank
 
-        def spread(cols, tag):
-            bank = psum.tile([P, 2, 2, P], F32, name=tag)
+        spreads = [("demand", 0), ("offset", 0), ("demand", 1), ("demand", 2), ("offset", 2), ("demand", 3)]
+
+        def B(b):
+            kind, i = spreads[b]
+            if kind == "demand":
+                cols = demand_cols[:, i, :].bitcast(F32)
+            else:
+                cols = offset_cols[:, i : i + 2, :].rearrange("p i a -> p (i a)").bitcast(F32)
+            bank = next_bank([P, 2, 2, P])
             for c in range(4):
                 nc.tensor.transpose(bank[:, c // 2, c % 2, :], cols[:, c : c + 1].to_broadcast([P, P]), ident[:])
-            return bank
+            t["spread", b] = bank
 
-        def spread_demand(i, tag, engine):
-            bank = spread(demand_cols[:, i, :].bitcast(F32), tag)
-            return lambda: copy_words(
-                engine,
-                demand_all[:, i, :].bitcast(F32).rearrange("p (h k a) -> p h k a", h=2, a=2),
-                bank[:].rearrange("p a h k -> p h k a"),
-            )
-
-        def spread_offset(i, tag, engine):
-            bank = spread(offset_cols[:, i : i + 2, :].rearrange("p i a -> p (i a)").bitcast(F32), tag)
-            return lambda: evac(engine, offset_all[:, i : i + 2, :].rearrange("p i d -> p (i d)"), bank)
+        def eb(b):
+            kind, i = spreads[b]
+            if kind == "demand":
+                copy_words(
+                    engine_of("eb", b),
+                    demand_all[:, i, :].bitcast(F32).rearrange("p (h k a) -> p h k a", h=2, a=2),
+                    t["spread", b][:].rearrange("p a h k -> p h k a"),
+                )
+            else:
+                evac(engine_of("eb", b), offset_all[:, i : i + 2, :].rearrange("p i d -> p (i d)"), t["spread", b])
 
         def yy(u):
             nc.vector.scalar_tensor_tensor(
@@ -228,7 +256,7 @@ def tile_ambulance_expected_coverage_k7_kernel(
             yb = work.tile([P, D], BF16, name="yb", align_bytes=64)
             dst = yb[:].rearrange("r (h p e) -> r h p e", h=2, e=2)
             src = y[:, u, :].rearrange("r (p h e) -> r h p e", h=2, e=2)
-            if True:
+            if engine_of("c", u) == "vector":
                 nc.vector.tensor_copy(out=dst, in_=src)
             else:
                 nc.scalar.copy(out=dst, in_=src)
@@ -236,18 +264,18 @@ def tile_ambulance_expected_coverage_k7_kernel(
 
         def T3(u):
             if u % 2 == 0:
-                t["y_bank"] = psum.tile([P, 2, 2, P], F32, name="y_bank")
+                t["y_bank", u // 2] = next_bank([P, 2, 2, P])
             words = t["yb", u][:].bitcast(F32)
             for h in range(2):
-                nc.tensor.transpose(t["y_bank"][:, u % 2, h, :], words[:, P * h : P * (h + 1)], ident[:])
+                nc.tensor.transpose(t["y_bank", u // 2][:, u % 2, h, :], words[:, P * h : P * (h + 1)], ident[:])
 
         def e3(u):
             if u % 2 == 1:
-                yt = work.tile([P, 2 * D], BF16, name="yt", align_bytes=64)
+                yt = work.tile([P, 2 * D], BF16, name="yt", bufs=3, align_bytes=64)
                 copy_words(
-                    "scalar",
+                    engine_of("e3", u),
                     yt[:].bitcast(F32).rearrange("p (r j h) -> p r j h", j=2, h=2),
-                    t["y_bank"][:].rearrange("p j h r -> p r j h"),
+                    t["y_bank", u // 2][:].rearrange("p j h r -> p r j h"),
                 )
                 t["yt", u] = yt
 
@@ -266,40 +294,47 @@ def tile_ambulance_expected_coverage_k7_kernel(
                     )
 
         order = [
-            (T1, 0),
-            (T2, 3),
-            (T3, 6),
-            (mult, 2),
-            (e1, 0),
-            (q1, 0),
-            (e2, 3),
-            (e3, 6),
-            (q2, 3),
-            (lambda u: M1(u, 0), 1),
-            (lambda u: sig(u, 0), 1),
-            (lambda u: M1(u, 1), 1),
-            (lambda u: sig(u, 1), 1),
-            (cast, 5),
-            (M2, 4),
-            (yy, 4),
-            (q3, 6),
+            (cast, 0, 8),
+            (T1, 1, 1),
+            (T3, 1, 9),
+            (e1, 0, 1),
+            (T2, 1, 4),
+            (yy, 0, 5),
+            (T2, 0, 3),
+            (cast, 1, 7),
+            (B, 0, 1),
+            (mult, 1, 3),
+            (e1, 1, 1),
+            (q1, 0, 1),
+            (q1, 1, 1),
+            (e2, 0, 3),
+            (M2, 1, 6),
+            (yy, 1, 6),
+            (e2, 1, 4),
+            (q2, 0, 3),
+            (lambda u: M1(u, 1), 0, 2),
+            (lambda u: M1(u, 0), 1, 2),
+            (lambda u: M1(u, 0), 0, 1),
+            (lambda u: sig(u, 1), 0, 2),
+            (eb, 0, 1),
+            (lambda u: M1(u, 1), 1, 2),
+            (q2, 1, 4),
+            (lambda u: sig(u, 0), 1, 2),
+            (e3, 1, 9),
+            (M2, 0, 4),
+            (lambda u: sig(u, 0), 0, 1),
+            (mult, 0, 2),
+            (T3, 0, 8),
+            (lambda u: sig(u, 1), 1, 2),
+            (T1, 0, 0),
+            (q3, 1, 9),
         ]
-        for step in range(UNITS + max(lag for stage, lag in order)):
-            late = []
-            for stage, lag in order:
-                if 0 <= step - lag < UNITS:
-                    stage(step - lag)
-                if stage is T1 and step in (0, 1, 2):
-                    engine = "vector" if step < 2 else "scalar"
-                    if step == 0:
-                        late = [spread_demand(0, "h_bank", engine)]
-                    elif step == 1:
-                        late = [spread_offset(0, "c_bank", engine), spread_demand(1, "y_bank", engine)]
-                    else:
-                        late = [
-                            spread_demand(2, "h_bank", engine),
-                            spread_offset(2, "c_bank", engine),
-                            spread_demand(3, "y_bank", engine),
-                        ]
-            for copy in late:
-                copy()
+        spread_step = [0,1,3,0,2,4]
+        for step in range(UNITS // 2 + max(lag for stage, j, lag in order) + 1):
+            for stage, j, lag in order:
+                if stage is B or stage is eb:
+                    for b in range(len(spreads)):
+                        if spread_step[b] == step - lag:
+                            stage(b)
+                elif 0 <= (step - lag) * 2 + j < UNITS:
+                    stage((step - lag) * 2 + j)

@@ -41,8 +41,8 @@ def tile_ambulance_expected_coverage_k7_kernel(
         v_scales = keep.tile([P, G * PASSES, D], U8, align_bytes=64)
         demand_all = keep.tile([P, G, Z], BF16, align_bytes=64)
         offset_all = keep.tile([P, G, D], BF16, align_bytes=64)
-        demand_cols = keep.tile([P, G, 8], BF16)
-        offset_cols = keep.tile([P, G, 4], BF16)
+        demand_cols = keep.tile([P, 2, 8], BF16)
+        offset_cols = keep.tile([P, 2, 4], BF16)
         staff_cols = keep.tile([P, UNITS // 2, 2], BF16)
         y = keep.tile([P, UNITS, D], F32, align_bytes=64)
         y_codes = keep.tile([P, G * R], U32, align_bytes=64)
@@ -74,6 +74,12 @@ def tile_ambulance_expected_coverage_k7_kernel(
                     in_=rows[:, first // 2 : (first + count) // 2].rearrange("p a j s -> p a (j s)"),
                 )
 
+        def load_spread(dst, rows):
+            nc.sync.dma_start(
+                out=dst[:, 2:G, :].rearrange("p i n -> p (i n)"),
+                in_=rows[2:G].rearrange("i n -> (i n)").partition_broadcast(P),
+            )
+
         def shifts(first, last):
             return slice(PASSES * first, PASSES * (last + 1))
 
@@ -84,13 +90,13 @@ def tile_ambulance_expected_coverage_k7_kernel(
 
         load_moves(0, 1)
         load_moves(1, 1)
-        nc.sync.dma_start(out=demand_cols[:], in_=demand.rearrange("i (k a) -> k i a", k=P))
+        nc.sync.dma_start(out=demand_cols[:], in_=demand[0:2].rearrange("i (k a) -> k i a", k=P))
         load_scales(w_scales, kern_scales, shifts(0, 0))
         load_words(w_words, kern_words, shifts(0, 0), slice(0, Z))
         load_words(w_words, kern_words, shifts(0, 0), slice(Z, 2 * Z))
         load_moves(2, 1)
         load_moves(3, 1)
-        nc.sync.dma_start(out=offset_cols[:], in_=offset.rearrange("i (k a) -> k i a", k=P))
+        nc.sync.dma_start(out=offset_cols[:], in_=offset[0:2].rearrange("i (k a) -> k i a", k=P))
         load_moves(4, 2)
         load_scales(w_scales, kern_scales, shifts(1, 1))
         load_words(w_words, kern_words, shifts(1, 1))
@@ -103,9 +109,11 @@ def tile_ambulance_expected_coverage_k7_kernel(
         load_words(w_words, kern_words, shifts(2, 2))
         load_words(v_words, weight_words, shifts(1, 1))
         load_moves(12, 4)
+        load_spread(demand_all, demand)
         load_words(w_words, kern_words, shifts(3, 3))
         load_scales(v_scales, weight_scales, shifts(2, 3))
         load_words(v_words, weight_words, shifts(2, 3))
+        load_spread(offset_all, offset)
 
         taken = []
 
@@ -114,7 +122,7 @@ def tile_ambulance_expected_coverage_k7_kernel(
             taken.append(bank)
             return bank
 
-        on_vector = {"e1": [0,3],"e2": [],"e3": [],"c": [1,3,5,7,9,11,13,15],"eb": [0,1,2,4,5]}
+        on_vector = {"e1": [2,3,7],"e2": [0],"e3": [13],"c": [0,2,4,6,8,10,13,14],"eb": [0,1,2]}
 
         def engine_of(stage, u):
             return "vector" if u in on_vector[stage] else "scalar"
@@ -177,7 +185,7 @@ def tile_ambulance_expected_coverage_k7_kernel(
 
         def sig(u, half):
             if half == 0:
-                t["sig", u] = work.tile([P, 2, PASSES, P, 2], F32, name="sig", align_bytes=64)
+                t["sig", u] = work.tile([P, 2, PASSES, P, 2], F32, name="sig", bufs=4, align_bytes=64)
             nc.scalar.activation(
                 out=t["sig", u][:, :, half, :, :],
                 in_=t["a_bank", u, half][:].rearrange("r (p h e) -> r h p e", h=2, e=2),
@@ -187,9 +195,9 @@ def tile_ambulance_expected_coverage_k7_kernel(
         def mult(u):
             hb = work.tile([P, Z], BF16, name="hb", bufs=7, align_bytes=64)
             nc.vector.tensor_tensor(
-                out=hb[:],
-                in0=t["sig", u][:].rearrange("r h g p e -> r (h g p e)"),
-                in1=demand_all[:, u // TILES, :],
+                out=hb[:].rearrange("r (h q e) -> r h q e", h=2, e=2),
+                in0=t["sig", u][:].rearrange("r h g p e -> r h (g p) e"),
+                in1=demand_all[:, u // TILES, :].rearrange("r (q h e) -> r h q e", h=2, e=2),
                 op=ALU.mult,
             )
             t["hb", u] = hb
@@ -216,7 +224,7 @@ def tile_ambulance_expected_coverage_k7_kernel(
             product(bank, t["hq", u], v_words, v_scales, u // TILES, slice(0, D))
             t["c_bank", u] = bank
 
-        spreads = [("demand", 0), ("offset", 0), ("demand", 1), ("demand", 2), ("offset", 2), ("demand", 3)]
+        spreads = [("demand", 0), ("offset", 0), ("demand", 1)]
 
         def B(b):
             kind, i = spreads[b]
@@ -234,8 +242,8 @@ def tile_ambulance_expected_coverage_k7_kernel(
             if kind == "demand":
                 copy_words(
                     engine_of("eb", b),
-                    demand_all[:, i, :].bitcast(F32).rearrange("p (h k a) -> p h k a", h=2, a=2),
-                    t["spread", b][:].rearrange("p a h k -> p h k a"),
+                    demand_all[:, i, :].bitcast(F32).rearrange("p (k c) -> p k c", c=4),
+                    t["spread", b][:].rearrange("p a h k -> p k (a h)"),
                 )
             else:
                 evac(engine_of("eb", b), offset_all[:, i : i + 2, :].rearrange("p i d -> p (i d)"), t["spread", b])
@@ -253,7 +261,7 @@ def tile_ambulance_expected_coverage_k7_kernel(
             nc.sync.dma_start(out=rows[:, u // 2, u % 2, :], in_=y[:, u, :])
 
         def cast(u):
-            yb = work.tile([P, D], BF16, name="yb", align_bytes=64)
+            yb = work.tile([P, D], BF16, name="yb", bufs=8, align_bytes=64)
             dst = yb[:].rearrange("r (h p e) -> r h p e", h=2, e=2)
             src = y[:, u, :].rearrange("r (p h e) -> r h p e", h=2, e=2)
             if engine_of("c", u) == "vector":
@@ -285,51 +293,51 @@ def tile_ambulance_expected_coverage_k7_kernel(
                 nc.vector.quantize_mx(out=y_codes[:, cols].bitcast(FP8X4), scales=y_scales[:, cols], in_=t["yt", u][:])
                 words = out_1[0].rearrange("p m t -> p (m t)").bitcast(I32)
                 nc.sync.dma_start(out=words[:, cols], in_=y_codes[:, cols].bitcast(I32))
-            if u % TILES == TILES - 1:
-                cols = slice(R * (u // TILES), R * (u // TILES + 1))
+            if u == UNITS - 1:
                 for q in range(4):
-                    nc.sync.dma_start(
-                        out=out_2[0, 4 * q : 4 * q + 4, cols].bitcast(I32),
-                        in_=y_scales[32 * q : 32 * q + 4, cols].bitcast(I32),
+                    queue = nc.scalar if q % 2 else nc.sync
+                    queue.dma_start(
+                        out=out_2[0, 4 * q : 4 * q + 4, :].bitcast(I32),
+                        in_=y_scales[32 * q : 32 * q + 4, :].bitcast(I32),
                     )
 
         order = [
-            (cast, 0, 8),
-            (T1, 1, 1),
-            (T3, 1, 9),
-            (e1, 0, 1),
-            (T2, 1, 4),
-            (yy, 0, 5),
-            (T2, 0, 3),
-            (cast, 1, 7),
+            (q3, 1, 10),
             (B, 0, 1),
-            (mult, 1, 3),
-            (e1, 1, 1),
-            (q1, 0, 1),
-            (q1, 1, 1),
-            (e2, 0, 3),
+            (cast, 0, 5),
             (M2, 1, 6),
-            (yy, 1, 6),
-            (e2, 1, 4),
-            (q2, 0, 3),
+            (mult, 1, 3),
             (lambda u: M1(u, 1), 0, 2),
-            (lambda u: M1(u, 0), 1, 2),
-            (lambda u: M1(u, 0), 0, 1),
-            (lambda u: sig(u, 1), 0, 2),
-            (eb, 0, 1),
-            (lambda u: M1(u, 1), 1, 2),
-            (q2, 1, 4),
-            (lambda u: sig(u, 0), 1, 2),
-            (e3, 1, 9),
+            (e2, 0, 3),
             (M2, 0, 4),
-            (lambda u: sig(u, 0), 0, 1),
-            (mult, 0, 2),
+            (lambda u: M1(u, 0), 1, 2),
+            (e1, 1, 1),
+            (e3, 1, 9),
+            (lambda u: M1(u, 1), 1, 2),
+            (lambda u: sig(u, 1), 0, 2),
+            (q1, 0, 1),
+            (lambda u: M1(u, 0), 0, 1),
+            (yy, 1, 6),
             (T3, 0, 8),
+            (T3, 1, 8),
+            (lambda u: sig(u, 0), 1, 2),
+            (cast, 1, 7),
+            (q2, 1, 4),
+            (eb, 0, 1),
             (lambda u: sig(u, 1), 1, 2),
+            (q2, 0, 3),
+            (yy, 0, 4),
+            (q1, 1, 1),
+            (lambda u: sig(u, 0), 0, 1),
+            (T2, 1, 3),
             (T1, 0, 0),
-            (q3, 1, 9),
+            (T1, 1, 0),
+            (mult, 0, 2),
+            (e1, 0, 0),
+            (T2, 0, 2),
+            (e2, 1, 3),
         ]
-        spread_step = [0,1,3,0,2,4]
+        spread_step = [0,1,0]
         for step in range(UNITS // 2 + max(lag for stage, j, lag in order) + 1):
             for stage, j, lag in order:
                 if stage is B or stage is eb:

from contextlib import ExitStack

import concourse.mybir as mybir
from concourse.masks import make_identity

G, R, S, Z, D = 4, 512, 1024, 1024, 512
FLOPS = 2 * G * R * (S * Z + Z * D)

F32 = mybir.dt.float32
BF16 = mybir.dt.bfloat16
I32 = mybir.dt.int32
U32 = mybir.dt.uint32
U8 = mybir.dt.uint8
FP8X4 = mybir.dt.float8_e4m3fn_x4
FP4X4 = mybir.dt.float4_e2m1fn_x4
ACT = mybir.ActivationFunctionType
ALU = mybir.AluOpType

P = 128
BANK = 512
TILES = R // P
UNITS = G * TILES
PASSES = 2


def tile_ambulance_expected_coverage_k7_kernel(
    tc, moves, kern_words, kern_scales, demand, weight_words, weight_scales, staffing, offset, out_0, out_1, out_2
):
    nc = tc.nc
    with ExitStack() as ctx:
        keep = ctx.enter_context(tc.tile_pool(name="keep", bufs=1))
        work = ctx.enter_context(tc.tile_pool(name="work", bufs=6))
        psum = ctx.enter_context(tc.psum_pool(name="psum", bufs=1))
        ctx.enter_context(tc.manual_schedule())

        ident = keep.tile([P, P], F32)
        mv = keep.tile([P, UNITS, S], BF16, align_bytes=64)
        w_words = keep.tile([P, G * PASSES, 2 * Z], U8, align_bytes=64)
        w_scales = keep.tile([P, G * PASSES, Z], U8, align_bytes=64)
        v_words = keep.tile([P, G * PASSES, 2 * D], U8, align_bytes=64)
        v_scales = keep.tile([P, G * PASSES, D], U8, align_bytes=64)
        demand_all = keep.tile([P, G, Z], BF16, align_bytes=64)
        offset_all = keep.tile([P, G, D], BF16, align_bytes=64)
        demand_cols = keep.tile([P, 2, 8], BF16)
        offset_cols = keep.tile([P, 2, 4], BF16)
        staff_cols = keep.tile([P, UNITS // 2, 2], BF16)
        y = keep.tile([P, UNITS, D], F32, align_bytes=64)
        y_codes = keep.tile([P, G * R], U32, align_bytes=64)
        y_scales = keep.tile([P, G * R], U8, align_bytes=64)

        def clear(plane, passes):
            nc.vector.memset(plane[:, passes, :].rearrange("p g n -> p (g n)").bitcast(I32), 0)

        def load_scales(plane, rows, passes):
            for q in range(4):
                nc.sync.dma_start(
                    out=plane[32 * q : 32 * q + 4, passes, :].bitcast(I32),
                    in_=rows[passes, 4 * q : 4 * q + 4, :].rearrange("g r n -> r g n").bitcast(I32),
                )

        def load_words(words, rows, passes, cols=slice(None)):
            nc.sync.dma_start(
                out=words[:, passes, cols].bitcast(I32),
                in_=rows[passes].rearrange("g p n -> p g n")[:, :, cols].bitcast(I32),
            )

        def load_moves(first, count):
            rows = moves.rearrange("i (a p j) s -> p (i a) j s", p=P, j=2)
            if count == 1:
                nc.sync.dma_start(out=mv[:, first, :], in_=rows[:, first // 2, first % 2, :])
            else:
                nc.sync.dma_start(
                    out=mv[:, first : first + count, :].rearrange("p (a j) s -> p a (j s)", j=2),
                    in_=rows[:, first // 2 : (first + count) // 2].rearrange("p a j s -> p a (j s)"),
                )

        def load_spread(dst, rows):
            nc.sync.dma_start(
                out=dst[:, 2:G, :].rearrange("p i n -> p (i n)"),
                in_=rows[2:G].rearrange("i n -> (i n)").partition_broadcast(P),
            )

        def shifts(first, last):
            return slice(PASSES * first, PASSES * (last + 1))

        make_identity(nc, ident[:])
        clear(w_scales, shifts(0, 0))
        clear(v_scales, shifts(0, 3))
        clear(w_scales, shifts(1, 3))

        load_moves(0, 1)
        load_moves(1, 1)
        nc.sync.dma_start(out=demand_cols[:], in_=demand[0:2].rearrange("i (k a) -> k i a", k=P))
        load_scales(w_scales, kern_scales, shifts(0, 0))
        load_words(w_words, kern_words, shifts(0, 0), slice(0, Z))
        load_words(w_words, kern_words, shifts(0, 0), slice(Z, 2 * Z))
        load_moves(2, 1)
        load_moves(3, 1)
        nc.sync.dma_start(out=offset_cols[:], in_=offset[0:2].rearrange("i (k a) -> k i a", k=P))
        load_moves(4, 2)
        load_scales(w_scales, kern_scales, shifts(1, 1))
        load_words(w_words, kern_words, shifts(1, 1))
        nc.sync.dma_start(out=staff_cols[:], in_=staffing.rearrange("i (a p j) -> p (i a) j", p=P, j=2))
        load_scales(v_scales, weight_scales, shifts(0, 1))
        load_words(v_words, weight_words, shifts(0, 0))
        load_moves(6, 2)
        load_moves(8, 4)
        load_scales(w_scales, kern_scales, shifts(2, 3))
        load_words(w_words, kern_words, shifts(2, 2))
        load_words(v_words, weight_words, shifts(1, 1))
        load_moves(12, 4)
        load_spread(demand_all, demand)
        load_words(w_words, kern_words, shifts(3, 3))
        load_scales(v_scales, weight_scales, shifts(2, 3))
        load_words(v_words, weight_words, shifts(2, 3))
        load_spread(offset_all, offset)

        taken = []

        def next_bank(shape):
            bank = psum.tile(shape, F32, name="bank%d" % (len(taken) % 8))
            taken.append(bank)
            return bank

        on_vector = {"e1": [2,3,7],"e2": [0],"e3": [13],"c": [0,2,4,6,8,10,13,14],"eb": [0,1,2]}

        def engine_of(stage, u):
            return "vector" if u in on_vector[stage] else "scalar"

        t = {}

        def T1(u):
            bank = next_bank([P, PASSES, 2, P])
            words = mv[:, u, :].bitcast(F32)
            for g in range(PASSES):
                for h in range(2):
                    nc.tensor.transpose(bank[:, g, h, :], words[:, 256 * g + h : 256 * (g + 1) : 2], ident[:])
            t["x_bank", u] = bank

        def evac(engine, dst, bank):
            copy_words(
                engine,
                dst.bitcast(F32).rearrange("p (g r h) -> p g r h", g=2, h=2),
                bank[:].rearrange("p g h r -> p g r h"),
            )

        def copy_words(engine, dst, src):
            if engine == "vector":
                nc.vector.tensor_copy(out=dst, in_=src)
            else:
                nc.scalar.copy(out=dst, in_=src)

        def e1(u):
            xt = work.tile([P, S], BF16, name="xt", align_bytes=64)
            evac(engine_of("e1", u), xt[:], t["x_bank", u])
            t["xt", u] = xt

        def quant(name, src):
            codes = work.tile([P, PASSES * P], U32, name=name + "_codes", align_bytes=64)
            scales = work.tile([P, PASSES * P], U8, name=name + "_scales", align_bytes=64)
            nc.vector.quantize_mx(out=codes[:].bitcast(FP8X4), scales=scales[:], in_=src[:])
            return codes, scales

        def q1(u):
            t["xq", u] = quant("x", t["xt", u])

        def product(bank, quantised, words, scales, shift, cols):
            codes, code_scales = quantised
            for g in range(PASSES):
                k = PASSES * shift + g
                nc.tensor.matmul_mx(
                    out=bank[:],
                    lhsT=codes[:, P * g : P * (g + 1)].bitcast(FP8X4),
                    lhsT_scale=code_scales[:, P * g : P * (g + 1)],
                    rhs=words[:, k, 2 * cols.start : 2 * cols.stop].bitcast(FP4X4),
                    rhs_scale=scales[:, k, cols],
                    start=(g == 0),
                    stop=(g == PASSES - 1),
                )

        def M1(u, half):
            bank = next_bank([P, BANK])
            product(bank, t["xq", u], w_words, w_scales, u // TILES, slice(BANK * half, BANK * (half + 1)))
            t["a_bank", u, half] = bank

        def sig(u, half):
            if half == 0:
                t["sig", u] = work.tile([P, 2, PASSES, P, 2], F32, name="sig", bufs=4, align_bytes=64)
            nc.scalar.activation(
                out=t["sig", u][:, :, half, :, :],
                in_=t["a_bank", u, half][:].rearrange("r (p h e) -> r h p e", h=2, e=2),
                func=ACT.Sigmoid,
            )

        def mult(u):
            hb = work.tile([P, Z], BF16, name="hb", bufs=7, align_bytes=64)
            nc.vector.tensor_tensor(
                out=hb[:].rearrange("r (h q e) -> r h q e", h=2, e=2),
                in0=t["sig", u][:].rearrange("r h g p e -> r h (g p) e"),
                in1=demand_all[:, u // TILES, :].rearrange("r (q h e) -> r h q e", h=2, e=2),
                op=ALU.mult,
            )
            t["hb", u] = hb

        def T2(u):
            bank = next_bank([P, PASSES, 2, P])
            words = t["hb", u][:].bitcast(F32)
            for g in range(PASSES):
                for h in range(2):
                    c = 256 * h + P * g
                    nc.tensor.transpose(bank[:, g, h, :], words[:, c : c + P], ident[:])
            t["h_bank", u] = bank

        def e2(u):
            ht = work.tile([P, Z], BF16, name="ht", align_bytes=64)
            evac(engine_of("e2", u), ht[:], t["h_bank", u])
            t["ht", u] = ht

        def q2(u):
            t["hq", u] = quant("h", t["ht", u])

        def M2(u):
            bank = next_bank([P, BANK])
            product(bank, t["hq", u], v_words, v_scales, u // TILES, slice(0, D))
            t["c_bank", u] = bank

        spreads = [("demand", 0), ("offset", 0), ("demand", 1)]

        def B(b):
            kind, i = spreads[b]
            if kind == "demand":
                cols = demand_cols[:, i, :].bitcast(F32)
            else:
                cols = offset_cols[:, i : i + 2, :].rearrange("p i a -> p (i a)").bitcast(F32)
            bank = next_bank([P, 2, 2, P])
            for c in range(4):
                nc.tensor.transpose(bank[:, c // 2, c % 2, :], cols[:, c : c + 1].to_broadcast([P, P]), ident[:])
            t["spread", b] = bank

        def eb(b):
            kind, i = spreads[b]
            if kind == "demand":
                copy_words(
                    engine_of("eb", b),
                    demand_all[:, i, :].bitcast(F32).rearrange("p (k c) -> p k c", c=4),
                    t["spread", b][:].rearrange("p a h k -> p k (a h)"),
                )
            else:
                evac(engine_of("eb", b), offset_all[:, i : i + 2, :].rearrange("p i d -> p (i d)"), t["spread", b])

        def yy(u):
            nc.vector.scalar_tensor_tensor(
                out=y[:, u, :],
                in0=t["c_bank", u][:],
                scalar=staff_cols[:, u // 2, u % 2 : u % 2 + 1],
                in1=offset_all[:, u // TILES, :],
                op0=ALU.mult,
                op1=ALU.add,
            )
            rows = out_0.rearrange("i (a p j) d -> p (i a) j d", p=P, j=2)
            nc.sync.dma_start(out=rows[:, u // 2, u % 2, :], in_=y[:, u, :])

        def cast(u):
            yb = work.tile([P, D], BF16, name="yb", bufs=8, align_bytes=64)
            dst = yb[:].rearrange("r (h p e) -> r h p e", h=2, e=2)
            src = y[:, u, :].rearrange("r (p h e) -> r h p e", h=2, e=2)
            if engine_of("c", u) == "vector":
                nc.vector.tensor_copy(out=dst, in_=src)
            else:
                nc.scalar.copy(out=dst, in_=src)
            t["yb", u] = yb

        def T3(u):
            if u % 2 == 0:
                t["y_bank", u // 2] = next_bank([P, 2, 2, P])
            words = t["yb", u][:].bitcast(F32)
            for h in range(2):
                nc.tensor.transpose(t["y_bank", u // 2][:, u % 2, h, :], words[:, P * h : P * (h + 1)], ident[:])

        def e3(u):
            if u % 2 == 1:
                yt = work.tile([P, 2 * D], BF16, name="yt", bufs=3, align_bytes=64)
                copy_words(
                    engine_of("e3", u),
                    yt[:].bitcast(F32).rearrange("p (r j h) -> p r j h", j=2, h=2),
                    t["y_bank", u // 2][:].rearrange("p j h r -> p r j h"),
                )
                t["yt", u] = yt

        def q3(u):
            if u % 2 == 1:
                cols = slice(P * (u - 1), P * (u + 1))
                nc.vector.quantize_mx(out=y_codes[:, cols].bitcast(FP8X4), scales=y_scales[:, cols], in_=t["yt", u][:])
                words = out_1[0].rearrange("p m t -> p (m t)").bitcast(I32)
                nc.sync.dma_start(out=words[:, cols], in_=y_codes[:, cols].bitcast(I32))
            if u == UNITS - 1:
                for q in range(4):
                    queue = nc.scalar if q % 2 else nc.sync
                    queue.dma_start(
                        out=out_2[0, 4 * q : 4 * q + 4, :].bitcast(I32),
                        in_=y_scales[32 * q : 32 * q + 4, :].bitcast(I32),
                    )

        order = [
            (q3, 1, 10),
            (B, 0, 1),
            (cast, 0, 5),
            (M2, 1, 6),
            (mult, 1, 3),
            (lambda u: M1(u, 1), 0, 2),
            (e2, 0, 3),
            (M2, 0, 4),
            (lambda u: M1(u, 0), 1, 2),
            (e1, 1, 1),
            (e3, 1, 9),
            (lambda u: M1(u, 1), 1, 2),
            (lambda u: sig(u, 1), 0, 2),
            (q1, 0, 1),
            (lambda u: M1(u, 0), 0, 1),
            (yy, 1, 6),
            (T3, 0, 8),
            (T3, 1, 8),
            (lambda u: sig(u, 0), 1, 2),
            (cast, 1, 7),
            (q2, 1, 4),
            (eb, 0, 1),
            (lambda u: sig(u, 1), 1, 2),
            (q2, 0, 3),
            (yy, 0, 4),
            (q1, 1, 1),
            (lambda u: sig(u, 0), 0, 1),
            (T2, 1, 3),
            (T1, 0, 0),
            (T1, 1, 0),
            (mult, 0, 2),
            (e1, 0, 0),
            (T2, 0, 2),
            (e2, 1, 3),
        ]
        spread_step = [0,1,0]
        for step in range(UNITS // 2 + max(lag for stage, j, lag in order) + 1):
            for stage, j, lag in order:
                if stage is B or stage is eb:
                    for b in range(len(spreads)):
                        if spread_step[b] == step - lag:
                            stage(b)
                elif 0 <= (step - lag) * 2 + j < UNITS:
                    stage((step - lag) * 2 + j)
